import numpy as np
import ml_dtypes


def mxq(x, axis, fmt="e4m3"):
    dtype, down = {"e4m3": (ml_dtypes.float8_e4m3fn, 7), "e5m2": (ml_dtypes.float8_e5m2, 14)}[fmt]
    v = np.moveaxis(np.asarray(x, np.float32).astype(ml_dtypes.bfloat16).astype(np.float64), axis, -1)
    blocks = v.reshape(v.shape[:-1] + (-1, 32))
    amax = np.abs(blocks).max(-1, keepdims=True)
    byte = np.maximum(np.where(amax > 0, np.frexp(amax)[1] - 1 + 127, 0) - down, 1)
    scale = np.exp2(byte - 127.0)
    codes = (blocks / scale).astype(np.float32).astype(dtype).astype(np.float64)
    return np.moveaxis((codes * scale).reshape(v.shape), -1, axis)


WIDE = False


def mx_kscale(k):
    if not WIDE:
        return np.ones(k)
    levels = np.array([10, -10, 5, -5, 0])
    if k % 512:
        return np.exp2(np.random.permutation(np.resize(levels, k // 32))).repeat(32)
    a = np.empty((k // 512, 16))
    for p in range(k // 512):
        a[p, :8] = np.random.permutation(np.resize(levels, 8))
        for g in range(8):
            far = levels[np.abs(levels - a[p, g]) >= 10]
            a[p, g + 8] = far[np.random.randint(len(far))]
    return np.exp2(a.ravel()).repeat(32)


def f64(x):
    return np.asarray(x).astype(np.float64)


def striped(idx):
    return np.tile(np.asarray(idx).reshape(-1, 16).T, (8, 1)).astype(np.uint16)


def unstriped(offs):
    return offs[:16].T.reshape(-1).astype(np.int64)


E2M1 = np.array([0.0, 0.5, 1.0, 1.5, 2.0, 3.0, 4.0, 6.0, -0.0, -0.5, -1.0, -1.5, -2.0, -3.0, -4.0, -6.0])


def pack_weight(w, fmt):
    k, n = w.shape
    w = f64(np.asarray(w, np.float32).astype(ml_dtypes.bfloat16)).reshape(k // 32, 32, n)
    amax = np.abs(w).max(1)
    if fmt == "e4m3":
        byte = np.frexp(amax)[1] - 1 + 127 - 7
    else:
        mant, ex = np.frexp(amax / 6.0)
        byte = np.where(mant > 0.5, ex, ex - 1) + 127
    byte = np.clip(np.where(amax > 0, byte, 1), 1, 254)
    scaled = (w * np.exp2(127.0 - byte)[:, None, :]).reshape(k, n).astype(np.float32)
    by_word = np.ascontiguousarray(scaled.reshape(k // 512, 128, 4, n).transpose(0, 1, 3, 2))
    if fmt == "e4m3":
        words = by_word.astype(ml_dtypes.float8_e4m3fn).view(np.uint8)
    else:
        c = by_word.astype(ml_dtypes.float4_e2m1fn).view(np.uint8) & 0xF
        words = (c[..., 0::2] | (c[..., 1::2] << 4)).reshape(k // 512, 128, 2 * n)
    return np.ascontiguousarray(words), np.ascontiguousarray(byte.astype(np.uint8).reshape(k // 512, 16, n))


def unpack_weight(words, scales, fmt):
    g, _, n = scales.shape
    words = np.ascontiguousarray(words).reshape(g, 128, n, -1)
    if fmt == "e4m3":
        vals = words.view(ml_dtypes.float8_e4m3fn).astype(np.float64)
    else:
        nib = np.empty((g, 128, n, 4), np.uint8)
        nib[..., 0::2] = words & 0xF
        nib[..., 1::2] = words >> 4
        vals = E2M1[nib]
    vals = vals * np.repeat(np.exp2(scales.astype(np.float64) - 127.0), 8, axis=1)[..., None]
    return vals.transpose(0, 1, 3, 2).reshape(g * 512, n)


def bf(x):
    return np.asarray(x, np.float32).astype(ml_dtypes.bfloat16)


def planes(Y):
    r, m = Y.shape
    b = f64(bf(Y)).reshape(r // 32, 32, m)
    amax = np.abs(b).max(1)
    byte = np.clip(np.where(amax > 0, np.frexp(amax)[1] - 1 + 127 - 7, 1), 1, 254)
    codes = (b * np.exp2(127.0 - byte)[:, None, :]).reshape(r, m).astype(np.float32).astype(ml_dtypes.float8_e4m3fn).view(np.uint8)
    words = codes.reshape(r // 512, 128, 4, m).transpose(0, 1, 3, 2)
    return np.ascontiguousarray(words), np.ascontiguousarray(byte.astype(np.uint8).reshape(r // 512, 16, m))


D, T, I, Q, E, U, Z = 512, 2048, 512, 256, 512, 1024, 1024


def setup_inputs():
    n = np.random.standard_normal
    idx = np.random.permutation(T)[:I]
    idx2 = np.random.permutation(U)[:I]
    idx3 = np.random.permutation(Z)[:I]
    fd = mx_kscale(D)
    fi = mx_kscale(I)
    ti = np.ones(T)
    ti[idx] = fi
    keysp = pack_weight(n((D, T)) / fd[:, None], "e2m1")
    return {
        "query": (n((D, Q)) * 0.6 / np.sqrt(D) * fd[:, None]).astype(np.float32),
        "query2": (n((D, Q)) * 0.6 / np.sqrt(D) * fd[:, None]).astype(np.float32),
        "query3": (n((D, Q)) * 0.6 / np.sqrt(D) * fd[:, None]).astype(np.float32),
        "keys_words": keysp[0],
        "keys_scales": keysp[1],
        "notes": (n((D, U)) / fd[:, None]).astype(np.float32),
        "pages": (n((D, Z)) / fd[:, None]).astype(np.float32),
        "os": (np.random.uniform(0.02, 0.08, (1, I)) * fi).astype(np.float32),
        "vals": (n((E, T)) / ti).astype(np.float32),
        "offs": striped(idx),
        "offs2": striped(idx2),
        "offs3": striped(idx3),
    }


def reference(query, query2, query3, keys_words, keys_scales, notes, pages, os, vals, offs, offs2, offs3):
    idx = unstriped(offs)
    idx2 = unstriped(offs2)
    idx3 = unstriped(offs3)
    keysu = unpack_weight(keys_words, keys_scales, "e2m1")
    queryq = mxq(f64(query), 0, "e4m3")
    keysidxg = keysu[:, idx]
    query2q = mxq(f64(query2), 0, "e4m3")
    notesidx2q = mxq(f64(notes)[:, idx2], 0, "e4m3")
    query3q = mxq(f64(query3), 0, "e4m3")
    pagesidx3q = mxq(f64(pages)[:, idx3], 0, "e4m3")
    s = queryq.T @ keysidxg + query2q.T @ notesidx2q + query3q.T @ pagesidx3q
    w = np.maximum(s, 0.0)
    wo1 = w * f64(os)
    wt1 = wo1.T
    vt1 = f64(vals)[:, idx].T
    vt1q = mxq(vt1, 0, "e4m3")
    wt1q = mxq(wt1, 0, "e4m3")
    o = vt1q.T @ wt1q
    words, scales = planes(o)
    return o, words, scales

@@ -1,0 +1,235 @@
+from contextlib import ExitStack
+
+import concourse.mybir as mybir
+from concourse.masks import make_identity
+
+D, T, I, Q, E, U, Z = 512, 2048, 512, 256, 512, 1024, 1024
+FLOPS = 2 * D * I * Q * 3 + 2 * I * E * Q
+
+F32 = mybir.dt.float32
+BF16 = mybir.dt.bfloat16
+I32 = mybir.dt.int32
+U32 = mybir.dt.uint32
+U16 = mybir.dt.uint16
+U8 = mybir.dt.uint8
+FP8X4 = mybir.dt.float8_e4m3fn_x4
+FP4X4 = mybir.dt.float4_e2m1fn_x4
+COPY = mybir.ActivationFunctionType.Copy
+MAX = mybir.AluOpType.max
+MULT = mybir.AluOpType.mult
+
+P = 128
+PACK = 4
+HALVES = 2
+QH = Q // HALVES
+LIST_COLS = I // 16
+
+
+def tile_attend_threesources_read_lean_pl_kernel(
+    tc, query, query2, query3, keys_words, keys_scales, notes, pages, slot_os, vals, offs, offs2, offs3, out_0, out_1, out_2
+):
+    nc = tc.nc
+    with ExitStack() as ctx:
+        lists = ctx.enter_context(tc.tile_pool(name="lists", bufs=1))
+        sb = ctx.enter_context(tc.tile_pool(name="sb", bufs=1))
+        value_space = ctx.enter_context(tc.tile_pool(name="value_space", bufs=1))
+        psum = ctx.enter_context(tc.psum_pool(name="psum", bufs=1))
+        turn_psum = ctx.enter_context(tc.psum_pool(name="turn_psum", bufs=2))
+
+        def load_list(name, source):
+            tile = lists.tile([P, LIST_COLS], U16, name=name)
+            nc.sync.dma_start(tile[:], source)
+            return tile
+
+        def load_plane(name, source, t, pool=sb, offset=None):
+            width = source.shape[1]
+            tile = pool.tile([P, width], F32, name="%s%d" % (name, t), offset=offset)
+            nc.sync.dma_start(tile[:], source.rearrange("(p t) c -> p t c", t=PACK)[:, t, :])
+            return tile
+
+        def load_query(name, source):
+            tile = sb.tile([P, PACK, Q], F32, name=name)
+            nc.sync.dma_start(tile[:], source.rearrange("(p t) q -> p t q", t=PACK))
+            return tile
+
+        def quantize(name, grouped, width):
+            codes = sb.tile([P, width], U32, name=name + "_codes", align_bytes=64)
+            scales = sb.tile([P, width], U8, name=name + "_scales", align_bytes=64)
+            nc.vector.quantize_mx(out=codes[:].bitcast(FP8X4), scales=scales[:], in_=grouped)
+            return codes, scales
+
+        def quantize_query(name, raw):
+            grouped = sb.tile([P, Q, PACK], BF16, name=name + "_grouped", align_bytes=64)
+            nc.scalar.copy(grouped[:], raw[:].rearrange("p t q -> p q t"))
+            return quantize(name, grouped[:].rearrange("p q t -> p (q t)"), Q)
+
+        def gather_on_vector(out, window, offsets):
+            nc.vector.tensor_copy(out, window[:].indirect(offsets))
+
+        def gather_on_scalar(out, window, offsets):
+            nc.scalar.activation(out, window[:].indirect(offsets), COPY)
+
+        def quantize_listed(name, planes, offsets, vector_parity):
+            picked = sb.tile([P, PACK, I], BF16, name=name + "_picked")
+            for t in range(PACK):
+                gather = gather_on_vector if t % 2 == vector_parity else gather_on_scalar
+                gather(picked[:, t, :], planes[t], offsets[:])
+            grouped = sb.tile([P, I, PACK], BF16, name=name + "_grouped", align_bytes=64)
+            nc.vector.tensor_copy(
+                grouped[:].rearrange("p (r c j) t -> p c r j t", r=PACK, j=2),
+                picked[:].rearrange("p t (c j r) -> p c r j t", r=PACK, j=2),
+            )
+            return quantize(name, grouped[:].rearrange("p i t -> p (i t)"), I)
+
+        key_scale_pool = sb.tile([P, T], U8, name="key_scale_pool")
+        nc.gpsimd.memset(key_scale_pool[:].bitcast(I32), 0)
+        identity = sb.tile([P, P], F32, name="identity")
+        make_identity(nc, identity[:])
+
+        def load_key_scales(quad):
+            nc.sync.dma_start(
+                key_scale_pool[32 * quad : 32 * quad + 4, :].bitcast(I32),
+                keys_scales[0, 4 * quad : 4 * quad + 4, :].bitcast(I32),
+            )
+
+        key_word_pool = sb.tile([P, T], U16, name="key_word_pool")
+        nc.sync.dma_start(key_word_pool[:].bitcast(I32), keys_words[0].bitcast(I32))
+        token_list = load_list("token_list", offs)
+        note_planes = [load_plane("notes", notes, 0)]
+        note_list = load_list("note_list", offs2)
+        for t in range(1, PACK):
+            note_planes.append(load_plane("notes", notes, t))
+            load_key_scales(t - 1)
+        query_raw = load_query("query_raw", query)
+        load_key_scales(3)
+        query2_raw = load_query("query2_raw", query2)
+        page_list = load_list("page_list", offs3)
+        page_planes = [load_plane("pages", pages, 0)]
+        factors = sb.tile([P, PACK], F32, name="factors")
+        nc.sync.dma_start(factors[:], slot_os.rearrange("o (p r) -> (o p) r", r=PACK))
+        page_planes.extend(load_plane("pages", pages, t) for t in range(1, PACK))
+        query3_raw = load_query("query3_raw", query3)
+        plane_bytes = 4 * T
+        value_planes = [load_plane("vals", vals, t, value_space, t * plane_bytes) for t in range(PACK)]
+
+        score_banks = [psum.tile([P, PACK, QH], F32, name="scores%d" % h) for h in range(HALVES)]
+
+        def score_passes(slot_codes, slot_dtype, slot_scales, query_codes, query_scales, first, last):
+            for h in range(HALVES):
+                q_cols = slice(h * QH, (h + 1) * QH)
+                for r in range(PACK):
+                    s_cols = slice(r * P, (r + 1) * P)
+                    nc.tensor.matmul_mx(
+                        out=score_banks[h][:, r, :],
+                        lhsT=slot_codes[:, s_cols].bitcast(slot_dtype),
+                        lhsT_scale=slot_scales[:, s_cols],
+                        rhs=query_codes[:, q_cols].bitcast(FP8X4),
+                        rhs_scale=query_scales[:, q_cols],
+                        start=(first and r == 0),
+                        stop=(last and r == PACK - 1),
+                    )
+
+        key_words_picked = sb.tile([P, I], U16, name="key_words_picked")
+        gather_on_vector(key_words_picked[:], key_word_pool, token_list[:])
+        key_scales = sb.tile([P, I], U8, name="key_scales", align_bytes=64)
+        gather_on_vector(key_scales[:].rearrange("p (r s) -> p s r", r=PACK), key_scale_pool, token_list[:])
+        key_words = sb.tile([P, I], U16, name="key_words", align_bytes=64)
+        nc.vector.tensor_copy(
+            key_words[:].rearrange("p (r c j) -> p c r j", r=PACK, j=8),
+            key_words_picked[:].rearrange("p (c j r) -> p c r j", r=PACK, j=8),
+        )
+        query_codes, query_scales = quantize_query("query", query_raw)
+        score_passes(key_words, FP4X4, key_scales, query_codes, query_scales, True, False)
+
+        note_codes, note_scales = quantize_listed("note", note_planes, note_list, 0)
+        query2_codes, query2_scales = quantize_query("query2", query2_raw)
+        score_passes(note_codes, FP8X4, note_scales, query2_codes, query2_scales, False, False)
+
+        page_codes, page_scales = quantize_listed("page", page_planes, page_list, 1)
+        query3_codes, query3_scales = quantize_query("query3", query3_raw)
+        score_passes(page_codes, FP8X4, page_scales, query3_codes, query3_scales, False, True)
+
+        weights = []
+        for h in range(HALVES):
+            grouped = sb.tile([P, QH, PACK], BF16, name="weight_grouped%d" % h, align_bytes=64)
+            nc.vector.scalar_tensor_tensor(
+                out=grouped[:],
+                in0=score_banks[h][:].rearrange("p r q -> p q r"),
+                scalar=0.0,
+                in1=factors[:].unsqueeze(1).to_broadcast([P, QH, PACK]),
+                op0=MAX,
+                op1=MULT,
+            )
+            weights.append(grouped)
+        weight_mx = [
+            quantize("weight%d" % h, weights[h][:].rearrange("p q r -> p (q r)"), QH) for h in range(HALVES)
+        ]
+
+        result_banks = [psum.tile([P, PACK, QH], F32, name="result%d" % h) for h in range(HALVES)]
+        out_rows = out_0.rearrange("(p t) q -> p t q", t=PACK)
+        half_cols = LIST_COLS // 2
+
+        def gather_and_turn(t):
+            picked = sb.tile([P, I], BF16, name="value_picked%d" % t)
+            gather_on_vector(picked[:, : I // 2], value_planes[t], token_list[:, :half_cols])
+            gather_on_scalar(picked[:, I // 2 :], value_planes[t], token_list[:, half_cols:])
+            pairs = picked[:].bitcast(F32)
+            turned = turn_psum.tile([P, 2, P], F32, name="turned")
+            for u in range(2):
+                nc.tensor.transpose(turned[:, u, :], pairs[:, u::2], identity[:])
+            return turned
+
+        def multiply(t, turned):
+            grouped = value_space.tile(
+                [P, P * PACK], BF16, name="value_grouped%d" % t, align_bytes=64, offset=(t + 1) * plane_bytes
+            )
+            nc.scalar.copy(
+                grouped[:].bitcast(F32).rearrange("p (e u) -> p e u", u=2), turned[:].rearrange("p u e -> p e u")
+            )
+            value_codes, value_scales = quantize("value%d" % t, grouped[:], P)
+            for h in range(HALVES):
+                nc.tensor.matmul_mx(
+                    out=result_banks[h][:, t, :],
+                    lhsT=value_codes[:].bitcast(FP8X4),
+                    lhsT_scale=value_scales[:],
+                    rhs=weight_mx[h][0][:].bitcast(FP8X4),
+                    rhs_scale=weight_mx[h][1][:],
+                    start=True,
+                    stop=True,
+                )
+
+        turned = gather_and_turn(0)
+        for t in range(1, PACK):
+            turned_next = gather_and_turn(t)
+            if t == PACK - 1:
+                early = value_space.tile([P, 2, Q], F32, name="early", offset=t * plane_bytes + 2 * P * PACK)
+                for h in range(HALVES):
+                    nc.vector.tensor_copy(early[:, :, h * QH : (h + 1) * QH], result_banks[h][:, 0:2, :])
+                nc.sync.dma_start(out_rows[:, 0:2, :], early[:])
+            multiply(t - 1, turned)
+            turned = turned_next
+        multiply(PACK - 1, turned)
+
+        rounded = [sb.tile([P, QH, PACK], BF16, name="rounded%d" % h, align_bytes=64) for h in range(HALVES)]
+        nc.scalar.copy(rounded[0][:], result_banks[0][:].rearrange("p t q -> p q t"))
+        nc.vector.tensor_copy(rounded[1][:], result_banks[1][:].rearrange("p t q -> p q t"))
+        late = sb.tile([P, 2, Q], F32, name="late")
+        for h in range(HALVES):
+            nc.scalar.copy(late[:, :, h * QH : (h + 1) * QH], result_banks[h][:, 2:4, :])
+        out_codes = sb.tile([P, Q], U32, name="out_codes", align_bytes=64)
+        out_scales = sb.tile([P, Q], U8, name="out_scales", align_bytes=64)
+        for h in range(HALVES):
+            q_cols = slice(h * QH, (h + 1) * QH)
+            nc.vector.quantize_mx(
+                out=out_codes[:, q_cols].bitcast(FP8X4),
+                scales=out_scales[:, q_cols],
+                in_=rounded[h][:].rearrange("p q t -> p (q t)"),
+            )
+        nc.sync.dma_start(out_rows[:, 2:4, :], late[:])
+        nc.sync.dma_start(out_1[0].rearrange("p q t -> p (q t)").bitcast(I32), out_codes[:].bitcast(I32))
+        for quad in range(4):
+            queue = nc.scalar if quad % 2 == 0 else nc.sync
+            queue.dma_start(
+                out_2[0, 4 * quad : 4 * quad + 4, :].bitcast(I32),
+                out_scales[32 * quad : 32 * quad + 4, :].bitcast(I32),
+            )

@@ -69,45 +69,49 @@ def tile_attend_threesources_read_lean_pl_kernel(
         def gather_on_scalar(out, window, offsets):
             nc.scalar.activation(out, window[:].indirect(offsets), COPY)
 
-        def quantize_listed(name, planes, offsets, vector_parity):
+        def gather_in_halves(out, window, offsets):
+            gather_on_vector(out[:, : I // 2], window, offsets[:, : LIST_COLS // 2])
+            gather_on_scalar(out[:, I // 2 :], window, offsets[:, LIST_COLS // 2 :])
+
+        def group_listed(name, planes, offsets):
             picked = sb.tile([P, PACK, I], BF16, name=name + "_picked")
             for t in range(PACK):
-                gather = gather_on_vector if t % 2 == vector_parity else gather_on_scalar
-                gather(picked[:, t, :], planes[t], offsets[:])
+                if t == PACK - 1:
+                    gather_in_halves(picked[:, t, :], planes[t], offsets)
+                else:
+                    gather = gather_on_vector if t == 1 else gather_on_scalar
+                    gather(picked[:, t, :], planes[t], offsets[:])
             grouped = sb.tile([P, I, PACK], BF16, name=name + "_grouped", align_bytes=64)
             nc.vector.tensor_copy(
                 grouped[:].rearrange("p (r c j) t -> p c r j t", r=PACK, j=2),
                 picked[:].rearrange("p t (c j r) -> p c r j t", r=PACK, j=2),
             )
-            return quantize(name, grouped[:].rearrange("p i t -> p (i t)"), I)
+            return grouped[:].rearrange("p i t -> p (i t)")
 
         key_scale_pool = sb.tile([P, T], U8, name="key_scale_pool")
         nc.gpsimd.memset(key_scale_pool[:].bitcast(I32), 0)
         identity = sb.tile([P, P], F32, name="identity")
         make_identity(nc, identity[:])
 
-        def load_key_scales(quad):
-            nc.sync.dma_start(
-                key_scale_pool[32 * quad : 32 * quad + 4, :].bitcast(I32),
-                keys_scales[0, 4 * quad : 4 * quad + 4, :].bitcast(I32),
-            )
+        def load_key_scales(j):
+            nc.sync.dma_start(key_scale_pool[j:P:32, :].bitcast(I32), keys_scales[0, j:16:4, :].bitcast(I32))
 
         key_word_pool = sb.tile([P, T], U16, name="key_word_pool")
         nc.sync.dma_start(key_word_pool[:].bitcast(I32), keys_words[0].bitcast(I32))
         token_list = load_list("token_list", offs)
-        note_planes = [load_plane("notes", notes, 0)]
-        note_list = load_list("note_list", offs2)
-        for t in range(1, PACK):
-            note_planes.append(load_plane("notes", notes, t))
-            load_key_scales(t - 1)
-        query_raw = load_query("query_raw", query)
-        load_key_scales(3)
         query2_raw = load_query("query2_raw", query2)
+        note_list = load_list("note_list", offs2)
+        note_planes = [load_plane("notes", notes, t) for t in range(2)]
+        for t in range(2, PACK):
+            load_key_scales(2 * t - 4)
+            load_key_scales(2 * t - 3)
+            note_planes.append(load_plane("notes", notes, t))
         page_list = load_list("page_list", offs3)
-        page_planes = [load_plane("pages", pages, 0)]
+        page_planes = [load_plane("pages", pages, t) for t in range(2)]
         factors = sb.tile([P, PACK], F32, name="factors")
         nc.sync.dma_start(factors[:], slot_os.rearrange("o (p r) -> (o p) r", r=PACK))
-        page_planes.extend(load_plane("pages", pages, t) for t in range(1, PACK))
+        page_planes.extend(load_plane("pages", pages, t) for t in range(2, PACK))
+        query_raw = load_query("query_raw", query)
         query3_raw = load_query("query3_raw", query3)
         plane_bytes = 4 * T
         value_planes = [load_plane("vals", vals, t, value_space, t * plane_bytes) for t in range(PACK)]
@@ -138,14 +142,16 @@ def tile_attend_threesources_read_lean_pl_kernel(
             key_words[:].rearrange("p (r c j) -> p c r j", r=PACK, j=8),
             key_words_picked[:].rearrange("p (c j r) -> p c r j", r=PACK, j=8),
         )
-        query_codes, query_scales = quantize_query("query", query_raw)
-        score_passes(key_words, FP4X4, key_scales, query_codes, query_scales, True, False)
 
-        note_codes, note_scales = quantize_listed("note", note_planes, note_list, 0)
         query2_codes, query2_scales = quantize_query("query2", query2_raw)
-        score_passes(note_codes, FP8X4, note_scales, query2_codes, query2_scales, False, False)
+        note_codes, note_scales = quantize("note", group_listed("note", note_planes, note_list), I)
+        score_passes(note_codes, FP8X4, note_scales, query2_codes, query2_scales, True, False)
 
-        page_codes, page_scales = quantize_listed("page", page_planes, page_list, 1)
+        page_grouped = group_listed("page", page_planes, page_list)
+        query_codes, query_scales = quantize_query("query", query_raw)
+        score_passes(key_words, FP4X4, key_scales, query_codes, query_scales, False, False)
+
+        page_codes, page_scales = quantize("page", page_grouped, I)
         query3_codes, query3_scales = quantize_query("query3", query3_raw)
         score_passes(page_codes, FP8X4, page_scales, query3_codes, query3_scales, False, True)
 
@@ -167,12 +173,10 @@ def tile_attend_threesources_read_lean_pl_kernel(
 
         result_banks = [psum.tile([P, PACK, QH], F32, name="result%d" % h) for h in range(HALVES)]
         out_rows = out_0.rearrange("(p t) q -> p t q", t=PACK)
-        half_cols = LIST_COLS // 2
 
         def gather_and_turn(t):
             picked = sb.tile([P, I], BF16, name="value_picked%d" % t)
-            gather_on_vector(picked[:, : I // 2], value_planes[t], token_list[:, :half_cols])
-            gather_on_scalar(picked[:, I // 2 :], value_planes[t], token_list[:, half_cols:])
+            gather_in_halves(picked[:], value_planes[t], token_list)
             pairs = picked[:].bitcast(F32)
             turned = turn_psum.tile([P, 2, P], F32, name="turned")
             for u in range(2):

@@ -47,6 +47,12 @@ def tile_attend_threesources_read_lean_pl_kernel(
             nc.sync.dma_start(tile[:], source.rearrange("(p t) c -> p t c", t=PACK)[:, t, :])
             return tile
 
+        def load_plane_pair(name, source, u):
+            width = source.shape[1]
+            tile = sb.tile([P, 2 * width], F32, name="%s%d" % (name, u))
+            nc.sync.dma_start(tile[:], source.rearrange("(p u e) c -> p u (e c)", u=2, e=2)[:, u, :])
+            return [tile[:, :width], tile[:, width:]]
+
         def load_query(name, source):
             tile = sb.tile([P, PACK, Q], F32, name=name)
             nc.sync.dma_start(tile[:], source.rearrange("(p t) q -> p t q", t=PACK))
@@ -64,27 +70,29 @@ def tile_attend_threesources_read_lean_pl_kernel(
             return quantize(name, grouped[:].rearrange("p q t -> p (q t)"), Q)
 
         def gather_on_vector(out, window, offsets):
-            nc.vector.tensor_copy(out, window[:].indirect(offsets))
+            nc.vector.tensor_copy(out, window.indirect(offsets))
 
         def gather_on_scalar(out, window, offsets):
-            nc.scalar.activation(out, window[:].indirect(offsets), COPY)
+            nc.scalar.activation(out, window.indirect(offsets), COPY)
 
         def gather_in_halves(out, window, offsets):
             gather_on_vector(out[:, : I // 2], window, offsets[:, : LIST_COLS // 2])
             gather_on_scalar(out[:, I // 2 :], window, offsets[:, LIST_COLS // 2 :])
 
-        def group_listed(name, planes, offsets):
-            picked = sb.tile([P, PACK, I], BF16, name=name + "_picked")
+        def whole_on_vector(out, window, offsets):
+            gather_on_vector(out, window, offsets[:])
+
+        def whole_on_scalar(out, window, offsets):
+            gather_on_scalar(out, window, offsets[:])
+
+        def group_listed(name, planes, offsets, gathers):
+            picked = sb.tile([P, PACK, I], F32, name=name + "_picked")
             for t in range(PACK):
-                if t == PACK - 1:
-                    gather_in_halves(picked[:, t, :], planes[t], offsets)
-                else:
-                    gather = gather_on_vector if t == 1 else gather_on_scalar
-                    gather(picked[:, t, :], planes[t], offsets[:])
+                gathers[t](picked[:, t, :], planes[t], offsets)
             grouped = sb.tile([P, I, PACK], BF16, name=name + "_grouped", align_bytes=64)
             nc.vector.tensor_copy(
-                grouped[:].rearrange("p (r c j) t -> p c r j t", r=PACK, j=2),
-                picked[:].rearrange("p t (c j r) -> p c r j t", r=PACK, j=2),
+                grouped[:].rearrange("p (r s) t -> p s r t", r=PACK),
+                picked[:].rearrange("p t (s r) -> p s r t", r=PACK),
             )
             return grouped[:].rearrange("p i t -> p (i t)")
 
@@ -101,17 +109,16 @@ def tile_attend_threesources_read_lean_pl_kernel(
         token_list = load_list("token_list", offs)
         query2_raw = load_query("query2_raw", query2)
         note_list = load_list("note_list", offs2)
-        note_planes = [load_plane("notes", notes, t) for t in range(2)]
-        for t in range(2, PACK):
-            load_key_scales(2 * t - 4)
-            load_key_scales(2 * t - 3)
-            note_planes.append(load_plane("notes", notes, t))
+        note_planes = load_plane_pair("notes", notes, 0)
+        for j in range(4):
+            load_key_scales(j)
+        note_planes.extend(load_plane_pair("notes", notes, 1))
+        query_raw = load_query("query_raw", query)
+        page_planes = load_plane_pair("pages", pages, 0)
         page_list = load_list("page_list", offs3)
-        page_planes = [load_plane("pages", pages, t) for t in range(2)]
+        page_planes.extend(load_plane_pair("pages", pages, 1))
         factors = sb.tile([P, PACK], F32, name="factors")
         nc.sync.dma_start(factors[:], slot_os.rearrange("o (p r) -> (o p) r", r=PACK))
-        page_planes.extend(load_plane("pages", pages, t) for t in range(2, PACK))
-        query_raw = load_query("query_raw", query)
         query3_raw = load_query("query3_raw", query3)
         plane_bytes = 4 * T
         value_planes = [load_plane("vals", vals, t, value_space, t * plane_bytes) for t in range(PACK)]
@@ -134,9 +141,9 @@ def tile_attend_threesources_read_lean_pl_kernel(
                     )
 
         key_words_picked = sb.tile([P, I], U16, name="key_words_picked")
-        gather_on_vector(key_words_picked[:], key_word_pool, token_list[:])
+        gather_on_vector(key_words_picked[:], key_word_pool[:], token_list[:])
         key_scales = sb.tile([P, I], U8, name="key_scales", align_bytes=64)
-        gather_on_vector(key_scales[:].rearrange("p (r s) -> p s r", r=PACK), key_scale_pool, token_list[:])
+        gather_on_vector(key_scales[:].rearrange("p (r s) -> p s r", r=PACK), key_scale_pool[:], token_list[:])
         key_words = sb.tile([P, I], U16, name="key_words", align_bytes=64)
         nc.vector.tensor_copy(
             key_words[:].rearrange("p (r c j) -> p c r j", r=PACK, j=8),
@@ -144,13 +151,13 @@ def tile_attend_threesources_read_lean_pl_kernel(
         )
 
         query2_codes, query2_scales = quantize_query("query2", query2_raw)
-        note_codes, note_scales = quantize("note", group_listed("note", note_planes, note_list), I)
+        note_codes, note_scales = quantize("note", group_listed("note", note_planes, note_list, (whole_on_scalar, whole_on_vector, whole_on_scalar, whole_on_vector)), I)
         score_passes(note_codes, FP8X4, note_scales, query2_codes, query2_scales, True, False)
 
-        page_grouped = group_listed("page", page_planes, page_list)
         query_codes, query_scales = quantize_query("query", query_raw)
         score_passes(key_words, FP4X4, key_scales, query_codes, query_scales, False, False)
 
+        page_grouped = group_listed("page", page_planes, page_list, (whole_on_scalar, gather_in_halves, whole_on_scalar, whole_on_vector))
         page_codes, page_scales = quantize("page", page_grouped, I)
         query3_codes, query3_scales = quantize_query("query3", query3_raw)
         score_passes(page_codes, FP8X4, page_scales, query3_codes, query3_scales, False, True)
@@ -176,26 +183,31 @@ def tile_attend_threesources_read_lean_pl_kernel(
 
         def gather_and_turn(t):
             picked = sb.tile([P, I], BF16, name="value_picked%d" % t)
-            gather_in_halves(picked[:], value_planes[t], token_list)
+            if t < 2:
+                gather_on_scalar(picked[:], value_planes[t][:], token_list[:])
+            else:
+                gather_in_halves(picked[:], value_planes[t][:], token_list)
             pairs = picked[:].bitcast(F32)
             turned = turn_psum.tile([P, 2, P], F32, name="turned")
             for u in range(2):
                 nc.tensor.transpose(turned[:, u, :], pairs[:, u::2], identity[:])
             return turned
 
-        def multiply(t, turned):
+        def quantize_values(t, turned):
             grouped = value_space.tile(
                 [P, P * PACK], BF16, name="value_grouped%d" % t, align_bytes=64, offset=(t + 1) * plane_bytes
             )
             nc.scalar.copy(
                 grouped[:].bitcast(F32).rearrange("p (e u) -> p e u", u=2), turned[:].rearrange("p u e -> p e u")
             )
-            value_codes, value_scales = quantize("value%d" % t, grouped[:], P)
+            return quantize("value%d" % t, grouped[:], P)
+
+        def multiply(t, value_mx):
             for h in range(HALVES):
                 nc.tensor.matmul_mx(
                     out=result_banks[h][:, t, :],
-                    lhsT=value_codes[:].bitcast(FP8X4),
-                    lhsT_scale=value_scales[:],
+                    lhsT=value_mx[0][:].bitcast(FP8X4),
+                    lhsT_scale=value_mx[1][:],
                     rhs=weight_mx[h][0][:].bitcast(FP8X4),
                     rhs_scale=weight_mx[h][1][:],
                     start=True,
@@ -205,14 +217,15 @@ def tile_attend_threesources_read_lean_pl_kernel(
         turned = gather_and_turn(0)
         for t in range(1, PACK):
             turned_next = gather_and_turn(t)
+            value_mx = quantize_values(t - 1, turned)
             if t == PACK - 1:
                 early = value_space.tile([P, 2, Q], F32, name="early", offset=t * plane_bytes + 2 * P * PACK)
-                for h in range(HALVES):
-                    nc.vector.tensor_copy(early[:, :, h * QH : (h + 1) * QH], result_banks[h][:, 0:2, :])
+                nc.vector.tensor_copy(early[:, :, :QH], result_banks[0][:, 0:2, :])
+                nc.scalar.copy(early[:, :, QH:], result_banks[1][:, 0:2, :])
                 nc.sync.dma_start(out_rows[:, 0:2, :], early[:])
-            multiply(t - 1, turned)
+            multiply(t - 1, value_mx)
             turned = turned_next
-        multiply(PACK - 1, turned)
+        multiply(PACK - 1, quantize_values(PACK - 1, turned))
 
         rounded = [sb.tile([P, QH, PACK], BF16, name="rounded%d" % h, align_bytes=64) for h in range(HALVES)]
         nc.scalar.copy(rounded[0][:], result_banks[0][:].rearrange("p t q -> p q t"))

@@ -3,8 +3,8 @@ from contextlib import ExitStack
 import concourse.mybir as mybir
 from concourse.masks import make_identity
 
-D, T, I, Q, E, U, Z = 512, 2048, 512, 256, 512, 1024, 1024
-FLOPS = 2 * D * I * Q * 3 + 2 * I * E * Q
+D, T, I, Q, E = 512, 2048, 512, 256, 512
+FLOPS = 3 * 2 * D * I * Q + 2 * I * E * Q
 
 F32 = mybir.dt.float32
 BF16 = mybir.dt.bfloat16
@@ -20,9 +20,14 @@ MULT = mybir.AluOpType.mult
 
 P = 128
 PACK = 4
+QUADRANT = 32
+SCALE_ROWS = 4
 HALVES = 2
 QH = Q // HALVES
 LIST_COLS = I // 16
+PLANE_BYTES = 4 * T
+GROUPED_BYTES = 2 * P * PACK
+EARLY_PLANES = 2
 
 
 def tile_attend_threesources_read_lean_pl_kernel(
@@ -41,10 +46,9 @@ def tile_attend_threesources_read_lean_pl_kernel(
             nc.sync.dma_start(tile[:], source)
             return tile
 
-        def load_plane(name, source, t, pool=sb, offset=None):
-            width = source.shape[1]
-            tile = pool.tile([P, width], F32, name="%s%d" % (name, t), offset=offset)
-            nc.sync.dma_start(tile[:], source.rearrange("(p t) c -> p t c", t=PACK)[:, t, :])
+        def load_value_plane(t):
+            tile = value_space.tile([P, T], F32, name="vals%d" % t, offset=t * PLANE_BYTES)
+            nc.sync.dma_start(tile[:], vals.rearrange("(p t) c -> p t c", t=PACK)[:, t, :])
             return tile
 
         def load_plane_pair(name, source, u):
@@ -79,16 +83,10 @@ def tile_attend_threesources_read_lean_pl_kernel(
             gather_on_vector(out[:, : I // 2], window, offsets[:, : LIST_COLS // 2])
             gather_on_scalar(out[:, I // 2 :], window, offsets[:, LIST_COLS // 2 :])
 
-        def whole_on_vector(out, window, offsets):
-            gather_on_vector(out, window, offsets[:])
-
-        def whole_on_scalar(out, window, offsets):
-            gather_on_scalar(out, window, offsets[:])
-
         def group_listed(name, planes, offsets, gathers):
             picked = sb.tile([P, PACK, I], F32, name=name + "_picked")
             for t in range(PACK):
-                gathers[t](picked[:, t, :], planes[t], offsets)
+                gathers[t](picked[:, t, :], planes[t], offsets[:])
             grouped = sb.tile([P, I, PACK], BF16, name=name + "_grouped", align_bytes=64)
             nc.vector.tensor_copy(
                 grouped[:].rearrange("p (r s) t -> p s r t", r=PACK),
@@ -101,17 +99,16 @@ def tile_attend_threesources_read_lean_pl_kernel(
         identity = sb.tile([P, P], F32, name="identity")
         make_identity(nc, identity[:])
 
-        def load_key_scales(j):
-            nc.sync.dma_start(key_scale_pool[j:P:32, :].bitcast(I32), keys_scales[0, j:16:4, :].bitcast(I32))
-
         key_word_pool = sb.tile([P, T], U16, name="key_word_pool")
         nc.sync.dma_start(key_word_pool[:].bitcast(I32), keys_words[0].bitcast(I32))
         token_list = load_list("token_list", offs)
         query2_raw = load_query("query2_raw", query2)
         note_list = load_list("note_list", offs2)
         note_planes = load_plane_pair("notes", notes, 0)
-        for j in range(4):
-            load_key_scales(j)
+        for j in range(SCALE_ROWS):
+            nc.sync.dma_start(
+                key_scale_pool[j:P:QUADRANT, :].bitcast(I32), keys_scales[0, j : D // 32 : SCALE_ROWS, :].bitcast(I32)
+            )
         note_planes.extend(load_plane_pair("notes", notes, 1))
         query_raw = load_query("query_raw", query)
         page_planes = load_plane_pair("pages", pages, 0)
@@ -120,8 +117,7 @@ def tile_attend_threesources_read_lean_pl_kernel(
         factors = sb.tile([P, PACK], F32, name="factors")
         nc.sync.dma_start(factors[:], slot_os.rearrange("o (p r) -> (o p) r", r=PACK))
         query3_raw = load_query("query3_raw", query3)
-        plane_bytes = 4 * T
-        value_planes = [load_plane("vals", vals, t, value_space, t * plane_bytes) for t in range(PACK)]
+        value_planes = [load_value_plane(t) for t in range(PACK)]
 
         score_banks = [psum.tile([P, PACK, QH], F32, name="scores%d" % h) for h in range(HALVES)]
 
@@ -150,15 +146,17 @@ def tile_attend_threesources_read_lean_pl_kernel(
             key_words_picked[:].rearrange("p (c j r) -> p c r j", r=PACK, j=8),
         )
 
+        note_gathers = (gather_on_scalar, gather_on_vector, gather_on_scalar, gather_in_halves)
+        page_gathers = (gather_on_scalar, gather_in_halves, gather_on_scalar, gather_on_vector)
+
         query2_codes, query2_scales = quantize_query("query2", query2_raw)
-        note_codes, note_scales = quantize("note", group_listed("note", note_planes, note_list, (whole_on_scalar, whole_on_vector, whole_on_scalar, whole_on_vector)), I)
+        note_codes, note_scales = quantize("note", group_listed("note", note_planes, note_list, note_gathers), I)
         score_passes(note_codes, FP8X4, note_scales, query2_codes, query2_scales, True, False)
 
         query_codes, query_scales = quantize_query("query", query_raw)
         score_passes(key_words, FP4X4, key_scales, query_codes, query_scales, False, False)
 
-        page_grouped = group_listed("page", page_planes, page_list, (whole_on_scalar, gather_in_halves, whole_on_scalar, whole_on_vector))
-        page_codes, page_scales = quantize("page", page_grouped, I)
+        page_codes, page_scales = quantize("page", group_listed("page", page_planes, page_list, page_gathers), I)
         query3_codes, query3_scales = quantize_query("query3", query3_raw)
         score_passes(page_codes, FP8X4, page_scales, query3_codes, query3_scales, False, True)
 
@@ -180,13 +178,11 @@ def tile_attend_threesources_read_lean_pl_kernel(
 
         result_banks = [psum.tile([P, PACK, QH], F32, name="result%d" % h) for h in range(HALVES)]
         out_rows = out_0.rearrange("(p t) q -> p t q", t=PACK)
+        value_gathers = (gather_on_scalar, gather_on_scalar, gather_in_halves, gather_in_halves)
 
         def gather_and_turn(t):
             picked = sb.tile([P, I], BF16, name="value_picked%d" % t)
-            if t < 2:
-                gather_on_scalar(picked[:], value_planes[t][:], token_list[:])
-            else:
-                gather_in_halves(picked[:], value_planes[t][:], token_list)
+            value_gathers[t](picked[:], value_planes[t][:], token_list[:])
             pairs = picked[:].bitcast(F32)
             turned = turn_psum.tile([P, 2, P], F32, name="turned")
             for u in range(2):
@@ -195,7 +191,7 @@ def tile_attend_threesources_read_lean_pl_kernel(
 
         def quantize_values(t, turned):
             grouped = value_space.tile(
-                [P, P * PACK], BF16, name="value_grouped%d" % t, align_bytes=64, offset=(t + 1) * plane_bytes
+                [P, P * PACK], BF16, name="value_grouped%d" % t, align_bytes=64, offset=(t + 1) * PLANE_BYTES
             )
             nc.scalar.copy(
                 grouped[:].bitcast(F32).rearrange("p (e u) -> p e u", u=2), turned[:].rearrange("p u e -> p e u")
@@ -219,10 +215,10 @@ def tile_attend_threesources_read_lean_pl_kernel(
             turned_next = gather_and_turn(t)
             value_mx = quantize_values(t - 1, turned)
             if t == PACK - 1:
-                early = value_space.tile([P, 2, Q], F32, name="early", offset=t * plane_bytes + 2 * P * PACK)
-                nc.vector.tensor_copy(early[:, :, :QH], result_banks[0][:, 0:2, :])
-                nc.scalar.copy(early[:, :, QH:], result_banks[1][:, 0:2, :])
-                nc.sync.dma_start(out_rows[:, 0:2, :], early[:])
+                early = value_space.tile([P, EARLY_PLANES, Q], F32, name="early", offset=t * PLANE_BYTES + GROUPED_BYTES)
+                for h in range(HALVES):
+                    nc.vector.tensor_copy(early[:, :, h * QH : (h + 1) * QH], result_banks[h][:, :EARLY_PLANES, :])
+                nc.sync.dma_start(out_rows[:, :EARLY_PLANES, :], early[:])
             multiply(t - 1, value_mx)
             turned = turned_next
         multiply(PACK - 1, quantize_values(PACK - 1, turned))
@@ -230,9 +226,9 @@ def tile_attend_threesources_read_lean_pl_kernel(
         rounded = [sb.tile([P, QH, PACK], BF16, name="rounded%d" % h, align_bytes=64) for h in range(HALVES)]
         nc.scalar.copy(rounded[0][:], result_banks[0][:].rearrange("p t q -> p q t"))
         nc.vector.tensor_copy(rounded[1][:], result_banks[1][:].rearrange("p t q -> p q t"))
-        late = sb.tile([P, 2, Q], F32, name="late")
+        late = sb.tile([P, PACK - EARLY_PLANES, Q], F32, name="late")
         for h in range(HALVES):
-            nc.scalar.copy(late[:, :, h * QH : (h + 1) * QH], result_banks[h][:, 2:4, :])
+            nc.scalar.copy(late[:, :, h * QH : (h + 1) * QH], result_banks[h][:, EARLY_PLANES:, :])
         out_codes = sb.tile([P, Q], U32, name="out_codes", align_bytes=64)
         out_scales = sb.tile([P, Q], U8, name="out_scales", align_bytes=64)
         for h in range(HALVES):
@@ -242,11 +238,11 @@ def tile_attend_threesources_read_lean_pl_kernel(
                 scales=out_scales[:, q_cols],
                 in_=rounded[h][:].rearrange("p q t -> p (q t)"),
             )
-        nc.sync.dma_start(out_rows[:, 2:4, :], late[:])
+        nc.sync.dma_start(out_rows[:, EARLY_PLANES:, :], late[:])
         nc.sync.dma_start(out_1[0].rearrange("p q t -> p (q t)").bitcast(I32), out_codes[:].bitcast(I32))
-        for quad in range(4):
+        for quad in range(P // QUADRANT):
             queue = nc.scalar if quad % 2 == 0 else nc.sync
             queue.dma_start(
-                out_2[0, 4 * quad : 4 * quad + 4, :].bitcast(I32),
-                out_scales[32 * quad : 32 * quad + 4, :].bitcast(I32),
+                out_2[0, SCALE_ROWS * quad : SCALE_ROWS * (quad + 1), :].bitcast(I32),
+                out_scales[QUADRANT * quad : QUADRANT * quad + SCALE_ROWS, :].bitcast(I32),
             )

from contextlib import ExitStack

import concourse.mybir as mybir
from concourse.masks import make_identity

D, T, I, Q, E = 512, 2048, 512, 256, 512
FLOPS = 3 * 2 * D * I * Q + 2 * I * E * Q

F32 = mybir.dt.float32
BF16 = mybir.dt.bfloat16
I32 = mybir.dt.int32
U32 = mybir.dt.uint32
U16 = mybir.dt.uint16
U8 = mybir.dt.uint8
FP8X4 = mybir.dt.float8_e4m3fn_x4
FP4X4 = mybir.dt.float4_e2m1fn_x4
COPY = mybir.ActivationFunctionType.Copy
MAX = mybir.AluOpType.max
MULT = mybir.AluOpType.mult

P = 128
PACK = 4
QUADRANT = 32
SCALE_ROWS = 4
HALVES = 2
QH = Q // HALVES
LIST_COLS = I // 16
PLANE_BYTES = 4 * T
GROUPED_BYTES = 2 * P * PACK
EARLY_PLANES = 2


def tile_attend_threesources_read_lean_pl_kernel(
    tc, query, query2, query3, keys_words, keys_scales, notes, pages, slot_os, vals, offs, offs2, offs3, out_0, out_1, out_2
):
    nc = tc.nc
    with ExitStack() as ctx:
        lists = ctx.enter_context(tc.tile_pool(name="lists", bufs=1))
        sb = ctx.enter_context(tc.tile_pool(name="sb", bufs=1))
        value_space = ctx.enter_context(tc.tile_pool(name="value_space", bufs=1))
        psum = ctx.enter_context(tc.psum_pool(name="psum", bufs=1))
        turn_psum = ctx.enter_context(tc.psum_pool(name="turn_psum", bufs=2))

        def load_list(name, source):
            tile = lists.tile([P, LIST_COLS], U16, name=name)
            nc.sync.dma_start(tile[:], source)
            return tile

        def load_value_plane(t):
            tile = value_space.tile([P, T], F32, name="vals%d" % t, offset=t * PLANE_BYTES)
            nc.sync.dma_start(tile[:], vals.rearrange("(p t) c -> p t c", t=PACK)[:, t, :])
            return tile

        def load_plane_pair(name, source, u):
            width = source.shape[1]
            tile = sb.tile([P, 2 * width], F32, name="%s%d" % (name, u))
            nc.sync.dma_start(tile[:], source.rearrange("(p u e) c -> p u (e c)", u=2, e=2)[:, u, :])
            return [tile[:, :width], tile[:, width:]]

        def load_query(name, source):
            tile = sb.tile([P, PACK, Q], F32, name=name)
            nc.sync.dma_start(tile[:], source.rearrange("(p t) q -> p t q", t=PACK))
            return tile

        def quantize(name, grouped, width):
            codes = sb.tile([P, width], U32, name=name + "_codes", align_bytes=64)
            scales = sb.tile([P, width], U8, name=name + "_scales", align_bytes=64)
            nc.vector.quantize_mx(out=codes[:].bitcast(FP8X4), scales=scales[:], in_=grouped)
            return codes, scales

        def quantize_query(name, raw):
            grouped = sb.tile([P, Q, PACK], BF16, name=name + "_grouped", align_bytes=64)
            nc.scalar.copy(grouped[:], raw[:].rearrange("p t q -> p q t"))
            return quantize(name, grouped[:].rearrange("p q t -> p (q t)"), Q)

        def gather_on_vector(out, window, offsets):
            nc.vector.tensor_copy(out, window.indirect(offsets))

        def gather_on_scalar(out, window, offsets):
            nc.scalar.activation(out, window.indirect(offsets), COPY)

        def gather_in_halves(out, window, offsets):
            gather_on_vector(out[:, : I // 2], window, offsets[:, : LIST_COLS // 2])
            gather_on_scalar(out[:, I // 2 :], window, offsets[:, LIST_COLS // 2 :])

        def group_listed(name, planes, offsets, gathers):
            picked = sb.tile([P, PACK, I], F32, name=name + "_picked")
            for t in range(PACK):
                gathers[t](picked[:, t, :], planes[t], offsets[:])
            grouped = sb.tile([P, I, PACK], BF16, name=name + "_grouped", align_bytes=64)
            nc.vector.tensor_copy(
                grouped[:].rearrange("p (r s) t -> p s r t", r=PACK),
                picked[:].rearrange("p t (s r) -> p s r t", r=PACK),
            )
            return grouped[:].rearrange("p i t -> p (i t)")

        key_scale_pool = sb.tile([P, T], U8, name="key_scale_pool")
        nc.gpsimd.memset(key_scale_pool[:].bitcast(I32), 0)
        identity = sb.tile([P, P], F32, name="identity")
        make_identity(nc, identity[:])

        key_word_pool = sb.tile([P, T], U16, name="key_word_pool")
        nc.sync.dma_start(key_word_pool[:].bitcast(I32), keys_words[0].bitcast(I32))
        token_list = load_list("token_list", offs)
        query2_raw = load_query("query2_raw", query2)
        note_list = load_list("note_list", offs2)
        note_planes = load_plane_pair("notes", notes, 0)
        for j in range(SCALE_ROWS):
            nc.sync.dma_start(
                key_scale_pool[j:P:QUADRANT, :].bitcast(I32), keys_scales[0, j : D // 32 : SCALE_ROWS, :].bitcast(I32)
            )
        note_planes.extend(load_plane_pair("notes", notes, 1))
        query_raw = load_query("query_raw", query)
        page_planes = load_plane_pair("pages", pages, 0)
        page_list = load_list("page_list", offs3)
        page_planes.extend(load_plane_pair("pages", pages, 1))
        factors = sb.tile([P, PACK], F32, name="factors")
        nc.sync.dma_start(factors[:], slot_os.rearrange("o (p r) -> (o p) r", r=PACK))
        query3_raw = load_query("query3_raw", query3)
        value_planes = [load_value_plane(t) for t in range(PACK)]

        score_banks = [psum.tile([P, PACK, QH], F32, name="scores%d" % h) for h in range(HALVES)]

        def score_passes(slot_codes, slot_dtype, slot_scales, query_codes, query_scales, first, last):
            for h in range(HALVES):
                q_cols = slice(h * QH, (h + 1) * QH)
                for r in range(PACK):
                    s_cols = slice(r * P, (r + 1) * P)
                    nc.tensor.matmul_mx(
                        out=score_banks[h][:, r, :],
                        lhsT=slot_codes[:, s_cols].bitcast(slot_dtype),
                        lhsT_scale=slot_scales[:, s_cols],
                        rhs=query_codes[:, q_cols].bitcast(FP8X4),
                        rhs_scale=query_scales[:, q_cols],
                        start=(first and r == 0),
                        stop=(last and r == PACK - 1),
                    )

        key_words_picked = sb.tile([P, I], U16, name="key_words_picked")
        gather_on_vector(key_words_picked[:], key_word_pool[:], token_list[:])
        key_scales = sb.tile([P, I], U8, name="key_scales", align_bytes=64)
        gather_on_vector(key_scales[:].rearrange("p (r s) -> p s r", r=PACK), key_scale_pool[:], token_list[:])
        key_words = sb.tile([P, I], U16, name="key_words", align_bytes=64)
        nc.vector.tensor_copy(
            key_words[:].rearrange("p (r c j) -> p c r j", r=PACK, j=8),
            key_words_picked[:].rearrange("p (c j r) -> p c r j", r=PACK, j=8),
        )

        note_gathers = (gather_on_scalar, gather_on_vector, gather_on_scalar, gather_in_halves)
        page_gathers = (gather_on_scalar, gather_in_halves, gather_on_scalar, gather_on_vector)

        query2_codes, query2_scales = quantize_query("query2", query2_raw)
        note_codes, note_scales = quantize("note", group_listed("note", note_planes, note_list, note_gathers), I)
        score_passes(note_codes, FP8X4, note_scales, query2_codes, query2_scales, True, False)

        query_codes, query_scales = quantize_query("query", query_raw)
        score_passes(key_words, FP4X4, key_scales, query_codes, query_scales, False, False)

        page_codes, page_scales = quantize("page", group_listed("page", page_planes, page_list, page_gathers), I)
        query3_codes, query3_scales = quantize_query("query3", query3_raw)
        score_passes(page_codes, FP8X4, page_scales, query3_codes, query3_scales, False, True)

        weights = []
        for h in range(HALVES):
            grouped = sb.tile([P, QH, PACK], BF16, name="weight_grouped%d" % h, align_bytes=64)
            nc.vector.scalar_tensor_tensor(
                out=grouped[:],
                in0=score_banks[h][:].rearrange("p r q -> p q r"),
                scalar=0.0,
                in1=factors[:].unsqueeze(1).to_broadcast([P, QH, PACK]),
                op0=MAX,
                op1=MULT,
            )
            weights.append(grouped)
        weight_mx = [
            quantize("weight%d" % h, weights[h][:].rearrange("p q r -> p (q r)"), QH) for h in range(HALVES)
        ]

        result_banks = [psum.tile([P, PACK, QH], F32, name="result%d" % h) for h in range(HALVES)]
        out_rows = out_0.rearrange("(p t) q -> p t q", t=PACK)
        value_gathers = (gather_on_scalar, gather_on_scalar, gather_in_halves, gather_in_halves)

        def gather_and_turn(t):
            picked = sb.tile([P, I], BF16, name="value_picked%d" % t)
            value_gathers[t](picked[:], value_planes[t][:], token_list[:])
            pairs = picked[:].bitcast(F32)
            turned = turn_psum.tile([P, 2, P], F32, name="turned")
            for u in range(2):
                nc.tensor.transpose(turned[:, u, :], pairs[:, u::2], identity[:])
            return turned

        def quantize_values(t, turned):
            grouped = value_space.tile(
                [P, P * PACK], BF16, name="value_grouped%d" % t, align_bytes=64, offset=(t + 1) * PLANE_BYTES
            )
            nc.scalar.copy(
                grouped[:].bitcast(F32).rearrange("p (e u) -> p e u", u=2), turned[:].rearrange("p u e -> p e u")
            )
            return quantize("value%d" % t, grouped[:], P)

        def multiply(t, value_mx):
            for h in range(HALVES):
                nc.tensor.matmul_mx(
                    out=result_banks[h][:, t, :],
                    lhsT=value_mx[0][:].bitcast(FP8X4),
                    lhsT_scale=value_mx[1][:],
                    rhs=weight_mx[h][0][:].bitcast(FP8X4),
                    rhs_scale=weight_mx[h][1][:],
                    start=True,
                    stop=True,
                )

        turned = gather_and_turn(0)
        for t in range(1, PACK):
            turned_next = gather_and_turn(t)
            value_mx = quantize_values(t - 1, turned)
            if t == PACK - 1:
                early = value_space.tile([P, EARLY_PLANES, Q], F32, name="early", offset=t * PLANE_BYTES + GROUPED_BYTES)
                for h in range(HALVES):
                    nc.vector.tensor_copy(early[:, :, h * QH : (h + 1) * QH], result_banks[h][:, :EARLY_PLANES, :])
                nc.sync.dma_start(out_rows[:, :EARLY_PLANES, :], early[:])
            multiply(t - 1, value_mx)
            turned = turned_next
        multiply(PACK - 1, quantize_values(PACK - 1, turned))

        rounded = [sb.tile([P, QH, PACK], BF16, name="rounded%d" % h, align_bytes=64) for h in range(HALVES)]
        nc.scalar.copy(rounded[0][:], result_banks[0][:].rearrange("p t q -> p q t"))
        nc.vector.tensor_copy(rounded[1][:], result_banks[1][:].rearrange("p t q -> p q t"))
        late = sb.tile([P, PACK - EARLY_PLANES, Q], F32, name="late")
        for h in range(HALVES):
            nc.scalar.copy(late[:, :, h * QH : (h + 1) * QH], result_banks[h][:, EARLY_PLANES:, :])
        out_codes = sb.tile([P, Q], U32, name="out_codes", align_bytes=64)
        out_scales = sb.tile([P, Q], U8, name="out_scales", align_bytes=64)
        for h in range(HALVES):
            q_cols = slice(h * QH, (h + 1) * QH)
            nc.vector.quantize_mx(
                out=out_codes[:, q_cols].bitcast(FP8X4),
                scales=out_scales[:, q_cols],
                in_=rounded[h][:].rearrange("p q t -> p (q t)"),
            )
        nc.sync.dma_start(out_rows[:, EARLY_PLANES:, :], late[:])
        nc.sync.dma_start(out_1[0].rearrange("p q t -> p (q t)").bitcast(I32), out_codes[:].bitcast(I32))
        for quad in range(P // QUADRANT):
            queue = nc.scalar if quad % 2 == 0 else nc.sync
            queue.dma_start(
                out_2[0, SCALE_ROWS * quad : SCALE_ROWS * (quad + 1), :].bitcast(I32),
                out_scales[QUADRANT * quad : QUADRANT * quad + SCALE_ROWS, :].bitcast(I32),
            )
